import numpy as np
import ml_dtypes


def mxq(x, axis, fmt="e4m3"):
    dtype, down = {"e4m3": (ml_dtypes.float8_e4m3fn, 7), "e5m2": (ml_dtypes.float8_e5m2, 14)}[fmt]
    v = np.moveaxis(np.asarray(x, np.float32).astype(ml_dtypes.bfloat16).astype(np.float64), axis, -1)
    blocks = v.reshape(v.shape[:-1] + (-1, 32))
    amax = np.abs(blocks).max(-1, keepdims=True)
    byte = np.maximum(np.where(amax > 0, np.frexp(amax)[1] - 1 + 127, 0) - down, 1)
    scale = np.exp2(byte - 127.0)
    codes = (blocks / scale).astype(np.float32).astype(dtype).astype(np.float64)
    return np.moveaxis((codes * scale).reshape(v.shape), -1, axis)


WIDE = False


def mx_kscale(k):
    if not WIDE:
        return np.ones(k)
    levels = np.array([30, -30])
    if k % 512:
        return np.exp2(np.random.permutation(np.resize(levels, k // 32))).repeat(32)
    a = np.empty((k // 512, 16))
    for p in range(k // 512):
        a[p, :8] = np.random.permutation(np.resize(levels, 8))
        for g in range(8):
            far = levels[np.abs(levels - a[p, g]) >= 10]
            a[p, g + 8] = far[np.random.randint(len(far))]
    return np.exp2(a.ravel()).repeat(32)


def f64(x):
    return np.asarray(x).astype(np.float64)


def striped(idx):
    return np.tile(np.asarray(idx).reshape(-1, 16).T, (8, 1)).astype(np.uint16)


def unstriped(offs):
    return offs[:16].T.reshape(-1).astype(np.int64)


E2M1 = np.array([0.0, 0.5, 1.0, 1.5, 2.0, 3.0, 4.0, 6.0, -0.0, -0.5, -1.0, -1.5, -2.0, -3.0, -4.0, -6.0])


def pack_weight(w, fmt):
    k, n = w.shape
    w = f64(np.asarray(w, np.float32).astype(ml_dtypes.bfloat16)).reshape(k // 32, 32, n)
    amax = np.abs(w).max(1)
    if fmt in ("e4m3", "e5m2"):
        byte = np.frexp(amax)[1] - 1 + 127 - (7 if fmt == "e4m3" else 14)
    else:
        mant, ex = np.frexp(amax / 6.0)
        byte = np.where(mant > 0.5, ex, ex - 1) + 127
    byte = np.clip(np.where(amax > 0, byte, 1), 1, 254)
    scaled = (w * np.exp2(127.0 - byte)[:, None, :]).reshape(k, n).astype(np.float32)
    by_word = np.ascontiguousarray(scaled.reshape(k // 512, 128, 4, n).transpose(0, 1, 3, 2))
    if fmt in ("e4m3", "e5m2"):
        words = by_word.astype(ml_dtypes.float8_e4m3fn if fmt == "e4m3" else ml_dtypes.float8_e5m2).view(np.uint8)
    else:
        c = by_word.astype(ml_dtypes.float4_e2m1fn).view(np.uint8) & 0xF
        words = (c[..., 0::2] | (c[..., 1::2] << 4)).reshape(k // 512, 128, 2 * n)
    return np.ascontiguousarray(words), np.ascontiguousarray(byte.astype(np.uint8).reshape(k // 512, 16, n))


def unpack_weight(words, scales, fmt):
    g, _, n = scales.shape
    words = np.ascontiguousarray(words).reshape(g, 128, n, -1)
    if fmt in ("e4m3", "e5m2"):
        vals = words.view(ml_dtypes.float8_e4m3fn if fmt == "e4m3" else ml_dtypes.float8_e5m2).astype(np.float64)
    else:
        nib = np.empty((g, 128, n, 4), np.uint8)
        nib[..., 0::2] = words & 0xF
        nib[..., 1::2] = words >> 4
        vals = E2M1[nib]
    vals = vals * np.repeat(np.exp2(scales.astype(np.float64) - 127.0), 8, axis=1)[..., None]
    return vals.transpose(0, 1, 3, 2).reshape(g * 512, n)


K, T, J, R, C, N, E = 512, 2048, 256, 512, 512, 256, 1024


def setup_inputs():
    n = np.random.standard_normal
    idx = np.random.permutation(T)[:J]
    idx2 = np.random.permutation(T)[:J]
    idx3 = np.random.permutation(C)[:J]
    idx4 = np.random.permutation(C)[:J]
    idx5 = np.random.permutation(E)[:J]
    fk = mx_kscale(K)
    fr = mx_kscale(R)
    xtp = pack_weight(n((K, T)) / fk[:, None], "e2m1")
    wp = pack_weight(n((K, R)) * 1 / np.sqrt(K) * fk[:, None] * fr, "e5m2")
    wbp = pack_weight(n((R, N)) * 1 / np.sqrt(R) / fr[:, None], "e4m3")
    wsp = pack_weight(n((K, N)) * 1 / np.sqrt(K) * fk[:, None], "e4m3")
    return {
        "xt_words": xtp[0],
        "xt_scales": xtp[1],
        "w_words": wp[0],
        "w_scales": wp[1],
        "wb_words": wbp[0],
        "wb_scales": wbp[1],
        "ws_words": wsp[0],
        "ws_scales": wsp[1],
        "tz": (n((N, E))).astype(np.float32),
        "offs": striped(idx),
        "offs2": striped(idx2),
        "offs3": striped(idx3),
        "offs4": striped(idx4),
        "offs5": striped(idx5),
    }


def reference(xt_words, xt_scales, w_words, w_scales, wb_words, wb_scales, ws_words, ws_scales, tz, offs, offs2, offs3, offs4, offs5):
    idx = unstriped(offs)
    idx2 = unstriped(offs2)
    idx3 = unstriped(offs3)
    idx4 = unstriped(offs4)
    idx5 = unstriped(offs5)
    xtu = unpack_weight(xt_words, xt_scales, "e2m1")
    wu = unpack_weight(w_words, w_scales, "e5m2")
    wbu = unpack_weight(wb_words, wb_scales, "e4m3")
    wsu = unpack_weight(ws_words, ws_scales, "e4m3")
    xtidxg = xtu[:, idx]
    a = wu.T @ xtidxg
    xtidx2g = xtu[:, idx2]
    b = wu.T @ xtidx2g
    pw = np.zeros((R, C))
    pw[:, idx3] = a
    hid = np.abs(pw[:, idx4] - b)
    hidq = mxq(hid, 0, "e5m2")
    p = wbu.T @ hidq + wsu.T @ xtidx2g
    y = p + f64(tz)[:, idx5]
    return y

@@ -1,0 +1,166 @@
+from contextlib import ExitStack
+
+import concourse.mybir as mybir
+
+K, T, J, R, C, N, E = 512, 2048, 256, 512, 512, 256, 1024
+FLOPS = 2 * K * R * J * 2 + 2 * R * N * J + 2 * K * N * J
+
+F32 = mybir.dt.float32
+BF16 = mybir.dt.bfloat16
+I32 = mybir.dt.int32
+U32 = mybir.dt.uint32
+U16 = mybir.dt.uint16
+U8 = mybir.dt.uint8
+E2M1 = mybir.dt.float4_e2m1fn_x4
+E4M3 = mybir.dt.float8_e4m3fn_x4
+E5M2 = mybir.dt.float8_e5m2_x4
+ACT = mybir.ActivationFunctionType
+ALU = mybir.AluOpType
+
+P = 128
+PACK = 4
+HALF = J // 2
+
+
+def load_plane(eng, plane, scales):
+    for q in range(4):
+        eng.dma_start(out=plane[32 * q : 32 * q + 4, :].bitcast(I32), in_=scales[0, 4 * q : 4 * q + 4, :].bitcast(I32))
+
+
+def words_of(dram):
+    return dram[0].rearrange("p n t -> p (n t)").bitcast(I32)
+
+
+def tile_list_tied_board_skip_tabled_kernel(
+    tc, xt_words, xt_scales, w_words, w_scales, wb_words, wb_scales, ws_words, ws_scales, tz,
+    offs, offs2, offs3, offs4, offs5, out,
+):
+    nc = tc.nc
+    with ExitStack() as ctx:
+        sb = ctx.enter_context(tc.tile_pool(name="sb", bufs=1))
+        ps = ctx.enter_context(tc.psum_pool(name="ps", bufs=1))
+
+        lists = [sb.tile([P, J // 16], U16, name="list%d" % i) for i in range(5)]
+        xw = sb.tile([P, T], U16, align_bytes=64)
+        xs = sb.tile([P, T], U8, align_bytes=64)
+        w_raw = sb.tile([P, R], U32, align_bytes=64)
+        wsc_raw = sb.tile([P, R], U8, align_bytes=64)
+        wb_w = sb.tile([P, N], U32, align_bytes=64)
+        wb_s = sb.tile([P, N], U8, align_bytes=64)
+        ws_w = sb.tile([P, N], U32, align_bytes=64)
+        ws_s = sb.tile([P, N], U8, align_bytes=64)
+        tz_sb = [sb.tile([P, E], F32, name="tz%d" % h) for h in range(2)]
+        boards = [sb.tile([P, C], F32, name="board%d" % t) for t in range(PACK)]
+
+        nc.vector.memset(wsc_raw[:].bitcast(I32), 0)
+        nc.vector.memset(xs[:, : T // 2].bitcast(I32), 0)
+        nc.gpsimd.memset(xs[:, T // 2 :].bitcast(I32), 0)
+        for t in range(PACK):
+            nc.vector.memset(boards[t][:], 0.0)
+        nc.vector.memset(ws_s[:].bitcast(I32), 0)
+        nc.vector.memset(wb_s[:].bitcast(I32), 0)
+
+        nc.sync.dma_start(lists[0][:], offs)
+        nc.sync.dma_start(lists[1][:], offs2)
+        load_plane(nc.sync, wsc_raw, w_scales)
+        nc.sync.dma_start(out=xw[:].bitcast(I32), in_=xt_words[0].bitcast(I32))
+        nc.sync.dma_start(out=w_raw[:].bitcast(I32), in_=words_of(w_words))
+        load_plane(nc.sync, xs, xt_scales)
+        nc.sync.dma_start(lists[2][:], offs3)
+        nc.sync.dma_start(lists[3][:], offs4)
+        nc.sync.dma_start(out=ws_w[:].bitcast(I32), in_=words_of(ws_words))
+        load_plane(nc.sync, ws_s, ws_scales)
+        nc.sync.dma_start(out=wb_w[:].bitcast(I32), in_=words_of(wb_words))
+        load_plane(nc.sync, wb_s, wb_scales)
+        nc.sync.dma_start(lists[4][:], offs5)
+        for h in range(2):
+            nc.sync.dma_start(out=tz_sb[h][:], in_=tz[h * P : (h + 1) * P, :])
+
+        w_w = sb.tile([P, PACK, P], U32, align_bytes=64)
+        w_s = sb.tile([P, PACK, P], U8, align_bytes=64)
+        nc.vector.tensor_copy(out=w_s[:], in_=wsc_raw[:].rearrange("p (m t) -> p t m", t=PACK))
+        nc.scalar.copy(out=w_w[:], in_=w_raw[:].rearrange("p (m t) -> p t m", t=PACK))
+
+        xgw = [sb.tile([P, J], U16, name="xgw%d" % i, align_bytes=64) for i in range(2)]
+        xgs = [sb.tile([P, J], U8, name="xgs%d" % i, align_bytes=64) for i in range(2)]
+
+        def pick_tokens(i):
+            nc.vector.tensor_copy(xgw[i][:], xw[:].indirect(lists[i][:]))
+            nc.vector.tensor_copy(xgs[i][:], xs[:].indirect(lists[i][:]))
+
+        pick_tokens(0)
+        a_sb = [sb.tile([P, J], F32, name="a_sb%d" % t) for t in range(PACK)]
+        a_ps = [ps.tile([P, J], F32, name="a_ps%d" % t) for t in range(PACK)]
+        for t in (0, 2, 3, 1):
+            nc.tensor.matmul_mx(
+                out=a_ps[t][:], lhsT=w_w[:, t, :].bitcast(E5M2), lhsT_scale=w_s[:, t, :],
+                rhs=xgw[0][:].bitcast(E2M1), rhs_scale=xgs[0][:], start=True, stop=True,
+            )
+        for t in (0, 2, 3):
+            nc.scalar.activation(a_sb[t][:], a_ps[t][:], ACT.Copy)
+
+        pick_tokens(1)
+        b_ps = [ps.tile([P, PACK, HALF], F32, name="b_ps%d" % h) for h in range(2)]
+        p_ps = [ps.tile([P, 2, HALF], F32, name="p_ps%d" % h) for h in range(2)]
+        for h in range(2):
+            cols = slice(h * HALF, (h + 1) * HALF)
+            for t in range(PACK):
+                nc.tensor.matmul_mx(
+                    out=b_ps[h][:, t, :], lhsT=w_w[:, t, :].bitcast(E5M2), lhsT_scale=w_s[:, t, :],
+                    rhs=xgw[1][:, cols].bitcast(E2M1), rhs_scale=xgs[1][:, cols], start=True, stop=True,
+                )
+        for h in range(2):
+            cols = slice(h * HALF, (h + 1) * HALF)
+            for n in range(2):
+                rows = slice(n * P, (n + 1) * P)
+                nc.tensor.matmul_mx(
+                    out=p_ps[h][:, n, :], lhsT=ws_w[:, rows].bitcast(E4M3), lhsT_scale=ws_s[:, rows],
+                    rhs=xgw[1][:, cols].bitcast(E2M1), rhs_scale=xgs[1][:, cols], start=(n == 0), stop=False,
+                )
+
+        looked = sb.tile([P, PACK, J], F32)
+        nc.vector.tensor_copy(boards[0][:].indirect(lists[2][:]), a_sb[0][:])
+        nc.vector.tensor_copy(a_sb[1][:], a_ps[1][:])
+        nc.vector.tensor_copy(boards[1][:].indirect(lists[2][:]), a_sb[1][:])
+        for t in (2, 3):
+            nc.scalar.activation(boards[t][:].indirect(lists[2][:]), a_sb[t][:], ACT.Copy)
+        for t in range(2):
+            nc.vector.tensor_copy(looked[:, t, :], boards[t][:].indirect(lists[3][:]))
+            nc.scalar.activation(looked[:, 2 + t, :], boards[2 + t][:].indirect(lists[3][:]), ACT.Copy)
+
+        def pick_table(h, tag):
+            picked = sb.tile([P, 2, HALF], F32, name="tzg%d" % h, tag=tag)
+            for n in range(2):
+                nc.scalar.activation(picked[:, n, :], tz_sb[n][:].indirect(lists[4][:, 8 * h : 8 * h + 8]), ACT.Copy)
+            return picked
+
+        tzg = [pick_table(0, "a_sb3")]
+        diff = [sb.tile([P, PACK, HALF], F32, name="diff%d" % h) for h in range(2)]
+        hid = [sb.tile([P, HALF, PACK], BF16, name="hid%d" % h, align_bytes=64) for h in range(2)]
+        for h in range(2):
+            cols = slice(h * HALF, (h + 1) * HALF)
+            nc.vector.tensor_tensor(diff[h][:], looked[:, :, cols], b_ps[h][:], ALU.subtract)
+            nc.scalar.activation(
+                hid[h][:].rearrange("p (c i) t -> p c t i", i=4),
+                diff[h][:].rearrange("p t (c i) -> p c t i", i=4),
+                ACT.Abs,
+            )
+        tzg.append(pick_table(1, "diff1"))
+        hq_w = [sb.tile([P, HALF], U32, name="hq_w%d" % h, align_bytes=64) for h in range(2)]
+        hq_s = [sb.tile([P, HALF], U8, name="hq_s%d" % h, align_bytes=64) for h in range(2)]
+        for h in range(2):
+            nc.vector.quantize_mx(
+                out=hq_w[h][:].bitcast(E5M2), scales=hq_s[h][:], in_=hid[h][:].rearrange("p j t -> p (j t)")
+            )
+            for n in range(2):
+                rows = slice(n * P, (n + 1) * P)
+                nc.tensor.matmul_mx(
+                    out=p_ps[h][:, n, :], lhsT=wb_w[:, rows].bitcast(E4M3), lhsT_scale=wb_s[:, rows],
+                    rhs=hq_w[h][:].bitcast(E5M2), rhs_scale=hq_s[h][:], start=False, stop=(n == 1),
+                )
+        out_v = out.rearrange("(n p) j -> p n j", p=P)
+        for h in range(2):
+            cols = slice(h * HALF, (h + 1) * HALF)
+            y = sb.tile([P, 2, HALF], F32, name="y%d" % h)
+            nc.vector.tensor_tensor(y[:], p_ps[h][:], tzg[h][:], ALU.add)
+            nc.sync.dma_start(out=out_v[:, :, cols], in_=y[:])

@@ -49,7 +49,7 @@ def tile_list_tied_board_skip_tabled_kernel(
         wb_s = sb.tile([P, N], U8, align_bytes=64)
         ws_w = sb.tile([P, N], U32, align_bytes=64)
         ws_s = sb.tile([P, N], U8, align_bytes=64)
-        tz_sb = [sb.tile([P, E], F32, name="tz%d" % h) for h in range(2)]
+        tz_sb = [sb.tile([P, E], F32, name="tz%d" % h, align_bytes=64) for h in range(2)]
         boards = [sb.tile([P, C], F32, name="board%d" % t) for t in range(PACK)]
 
         nc.vector.memset(wsc_raw[:].bitcast(I32), 0)
@@ -57,8 +57,8 @@ def tile_list_tied_board_skip_tabled_kernel(
         nc.gpsimd.memset(xs[:, T // 2 :].bitcast(I32), 0)
         for t in range(PACK):
             nc.vector.memset(boards[t][:], 0.0)
-        nc.vector.memset(ws_s[:].bitcast(I32), 0)
-        nc.vector.memset(wb_s[:].bitcast(I32), 0)
+        nc.gpsimd.memset(ws_s[:].bitcast(I32), 0)
+        nc.gpsimd.memset(wb_s[:].bitcast(I32), 0)
 
         nc.sync.dma_start(lists[0][:], offs)
         nc.sync.dma_start(lists[1][:], offs2)
@@ -68,18 +68,22 @@ def tile_list_tied_board_skip_tabled_kernel(
         load_plane(nc.sync, xs, xt_scales)
         nc.sync.dma_start(lists[2][:], offs3)
         nc.sync.dma_start(lists[3][:], offs4)
-        nc.sync.dma_start(out=ws_w[:].bitcast(I32), in_=words_of(ws_words))
-        load_plane(nc.sync, ws_s, ws_scales)
-        nc.sync.dma_start(out=wb_w[:].bitcast(I32), in_=words_of(wb_words))
-        load_plane(nc.sync, wb_s, wb_scales)
         nc.sync.dma_start(lists[4][:], offs5)
-        for h in range(2):
-            nc.sync.dma_start(out=tz_sb[h][:], in_=tz[h * P : (h + 1) * P, :])
+        nc.sync.dma_start(out=tz_sb[0][:], in_=tz[0:P, :])
+        nc.sync.dma_start(out=ws_w[:].bitcast(I32), in_=words_of(ws_words))
+        nc.sync.dma_start(out=wb_w[:].bitcast(I32), in_=words_of(wb_words))
+        load_plane(nc.sync, ws_s, ws_scales)
+        load_plane(nc.sync, wb_s, wb_scales)
+        nc.sync.dma_start(out=tz_sb[1][:], in_=tz[P : 2 * P, :])
 
-        w_w = sb.tile([P, PACK, P], U32, align_bytes=64)
+        w_w = [sb.tile([P, 2, P], U32, name="w_w%d" % u, align_bytes=64) for u in range(2)]
         w_s = sb.tile([P, PACK, P], U8, align_bytes=64)
         nc.vector.tensor_copy(out=w_s[:], in_=wsc_raw[:].rearrange("p (m t) -> p t m", t=PACK))
-        nc.scalar.copy(out=w_w[:], in_=w_raw[:].rearrange("p (m t) -> p t m", t=PACK))
+        for u in range(2):
+            nc.scalar.copy(
+                out=w_w[u][:].rearrange("p t (c i) -> p c t i", i=4),
+                in_=w_raw[:].rearrange("p (c i t) -> p c t i", i=4, t=PACK)[:, :, 2 * u : 2 * u + 2, :],
+            )
 
         xgw = [sb.tile([P, J], U16, name="xgw%d" % i, align_bytes=64) for i in range(2)]
         xgs = [sb.tile([P, J], U8, name="xgs%d" % i, align_bytes=64) for i in range(2)]
@@ -91,24 +95,22 @@ def tile_list_tied_board_skip_tabled_kernel(
         pick_tokens(0)
         a_sb = [sb.tile([P, J], F32, name="a_sb%d" % t) for t in range(PACK)]
         a_ps = [ps.tile([P, J], F32, name="a_ps%d" % t) for t in range(PACK)]
-        for t in (0, 2, 3, 1):
+        for t in (0, 1, 3, 2):
             nc.tensor.matmul_mx(
-                out=a_ps[t][:], lhsT=w_w[:, t, :].bitcast(E5M2), lhsT_scale=w_s[:, t, :],
+                out=a_ps[t][:], lhsT=w_w[t // 2][:, t % 2, :].bitcast(E5M2), lhsT_scale=w_s[:, t, :],
                 rhs=xgw[0][:].bitcast(E2M1), rhs_scale=xgs[0][:], start=True, stop=True,
             )
-        for t in (0, 2, 3):
+        for t in (0, 1, 3):
             nc.scalar.activation(a_sb[t][:], a_ps[t][:], ACT.Copy)
 
         pick_tokens(1)
-        b_ps = [ps.tile([P, PACK, HALF], F32, name="b_ps%d" % h) for h in range(2)]
+        b_ps = [ps.tile([P, 2, J], F32, name="b_ps%d" % e) for e in range(2)]
         p_ps = [ps.tile([P, 2, HALF], F32, name="p_ps%d" % h) for h in range(2)]
-        for h in range(2):
-            cols = slice(h * HALF, (h + 1) * HALF)
-            for t in range(PACK):
-                nc.tensor.matmul_mx(
-                    out=b_ps[h][:, t, :], lhsT=w_w[:, t, :].bitcast(E5M2), lhsT_scale=w_s[:, t, :],
-                    rhs=xgw[1][:, cols].bitcast(E2M1), rhs_scale=xgs[1][:, cols], start=True, stop=True,
-                )
+        for t in range(PACK):
+            nc.tensor.matmul_mx(
+                out=b_ps[t % 2][:, t // 2, :], lhsT=w_w[t // 2][:, t % 2, :].bitcast(E5M2), lhsT_scale=w_s[:, t, :],
+                rhs=xgw[1][:].bitcast(E2M1), rhs_scale=xgs[1][:], start=True, stop=True,
+            )
         for h in range(2):
             cols = slice(h * HALF, (h + 1) * HALF)
             for n in range(2):
@@ -118,35 +120,42 @@ def tile_list_tied_board_skip_tabled_kernel(
                     rhs=xgw[1][:, cols].bitcast(E2M1), rhs_scale=xgs[1][:, cols], start=(n == 0), stop=False,
                 )
 
-        looked = sb.tile([P, PACK, J], F32)
+        looked = [sb.tile([P, 2, J], F32, name="looked%d" % e) for e in range(2)]
         nc.vector.tensor_copy(boards[0][:].indirect(lists[2][:]), a_sb[0][:])
-        nc.vector.tensor_copy(a_sb[1][:], a_ps[1][:])
-        nc.vector.tensor_copy(boards[1][:].indirect(lists[2][:]), a_sb[1][:])
-        for t in (2, 3):
+        nc.vector.tensor_copy(a_sb[2][:], a_ps[2][:])
+        nc.vector.tensor_copy(boards[2][:].indirect(lists[2][:]), a_sb[2][:])
+        for t in (1, 3):
             nc.scalar.activation(boards[t][:].indirect(lists[2][:]), a_sb[t][:], ACT.Copy)
-        for t in range(2):
-            nc.vector.tensor_copy(looked[:, t, :], boards[t][:].indirect(lists[3][:]))
-            nc.scalar.activation(looked[:, 2 + t, :], boards[2 + t][:].indirect(lists[3][:]), ACT.Copy)
+        for u in range(2):
+            nc.vector.tensor_copy(looked[0][:, u, :], boards[2 * u][:].indirect(lists[3][:]))
+            nc.scalar.activation(looked[1][:, u, :], boards[2 * u + 1][:].indirect(lists[3][:]), ACT.Copy)
 
-        def pick_table(h, tag):
-            picked = sb.tile([P, 2, HALF], F32, name="tzg%d" % h, tag=tag)
-            for n in range(2):
-                nc.scalar.activation(picked[:, n, :], tz_sb[n][:].indirect(lists[4][:, 8 * h : 8 * h + 8]), ACT.Copy)
-            return picked
-
-        tzg = [pick_table(0, "a_sb3")]
-        diff = [sb.tile([P, PACK, HALF], F32, name="diff%d" % h) for h in range(2)]
-        hid = [sb.tile([P, HALF, PACK], BF16, name="hid%d" % h, align_bytes=64) for h in range(2)]
+        tzg = sb.tile([P, 2, J], F32, tag="board3")
+        nc.scalar.activation(tzg[:, 0, :], tz_sb[0][:].indirect(lists[4][:]), ACT.Copy)
+        diff = sb.tile([P, 2, 2, 2, HALF], F32)
+        hid = [
+            sb.tile([P, HALF, PACK], BF16, name="hid0", tag="tz0", align_bytes=64),
+            sb.tile([P, HALF, PACK], BF16, name="hid1", align_bytes=64),
+        ]
+        nc.vector.tensor_tensor(
+            diff[:, :, :, 0, :],
+            looked[0][:].rearrange("p u (h j) -> p h u j", h=2),
+            b_ps[0][:].rearrange("p u (h j) -> p h u j", h=2),
+            ALU.subtract,
+        )
         for h in range(2):
             cols = slice(h * HALF, (h + 1) * HALF)
-            nc.vector.tensor_tensor(diff[h][:], looked[:, :, cols], b_ps[h][:], ALU.subtract)
+            nc.vector.tensor_tensor(diff[:, h, :, 1, :], looked[1][:, :, cols], b_ps[1][:, :, cols], ALU.subtract)
             nc.scalar.activation(
                 hid[h][:].rearrange("p (c i) t -> p c t i", i=4),
-                diff[h][:].rearrange("p t (c i) -> p c t i", i=4),
+                diff[:, h, :, :, :].rearrange("p u e (c i) -> p c (u e) i", i=4),
                 ACT.Abs,
             )
-        tzg.append(pick_table(1, "diff1"))
-        hq_w = [sb.tile([P, HALF], U32, name="hq_w%d" % h, align_bytes=64) for h in range(2)]
+        nc.vector.tensor_copy(tzg[:, 1, :], tz_sb[1][:].indirect(lists[4][:]))
+        hq_w = [
+            sb.tile([P, HALF], U32, name="hq_w0", tag="tz1", align_bytes=64),
+            sb.tile([P, HALF], U32, name="hq_w1", align_bytes=64),
+        ]
         hq_s = [sb.tile([P, HALF], U8, name="hq_s%d" % h, align_bytes=64) for h in range(2)]
         for h in range(2):
             nc.vector.quantize_mx(
@@ -161,6 +170,6 @@ def tile_list_tied_board_skip_tabled_kernel(
         out_v = out.rearrange("(n p) j -> p n j", p=P)
         for h in range(2):
             cols = slice(h * HALF, (h + 1) * HALF)
-            y = sb.tile([P, 2, HALF], F32, name="y%d" % h)
-            nc.vector.tensor_tensor(y[:], p_ps[h][:], tzg[h][:], ALU.add)
+            y = sb.tile([P, 2, HALF], F32, name="y%d" % h, tag="hid1" if h == 0 else "y1", align_bytes=64)
+            nc.vector.tensor_tensor(y[:], p_ps[h][:], tzg[:, :, cols], ALU.add)
             nc.sync.dma_start(out=out_v[:, :, cols], in_=y[:])

@@ -69,12 +69,12 @@ def tile_list_tied_board_skip_tabled_kernel(
         nc.sync.dma_start(lists[2][:], offs3)
         nc.sync.dma_start(lists[3][:], offs4)
         nc.sync.dma_start(lists[4][:], offs5)
-        nc.sync.dma_start(out=tz_sb[0][:], in_=tz[0:P, :])
+        for n in range(2):
+            nc.sync.dma_start(out=tz_sb[n][:], in_=tz[n * P : (n + 1) * P, :])
         nc.sync.dma_start(out=ws_w[:].bitcast(I32), in_=words_of(ws_words))
         nc.sync.dma_start(out=wb_w[:].bitcast(I32), in_=words_of(wb_words))
         load_plane(nc.sync, ws_s, ws_scales)
         load_plane(nc.sync, wb_s, wb_scales)
-        nc.sync.dma_start(out=tz_sb[1][:], in_=tz[P : 2 * P, :])
 
         w_w = [sb.tile([P, 2, P], U32, name="w_w%d" % u, align_bytes=64) for u in range(2)]
         w_s = sb.tile([P, PACK, P], U8, align_bytes=64)
@@ -82,7 +82,7 @@ def tile_list_tied_board_skip_tabled_kernel(
         for u in range(2):
             nc.scalar.copy(
                 out=w_w[u][:].rearrange("p t (c i) -> p c t i", i=4),
-                in_=w_raw[:].rearrange("p (c i t) -> p c t i", i=4, t=PACK)[:, :, 2 * u : 2 * u + 2, :],
+                in_=w_raw[:].rearrange("p (c i v e) -> p e c v i", i=4, v=2, e=2)[:, u, :, :, :],
             )
 
         xgw = [sb.tile([P, J], U16, name="xgw%d" % i, align_bytes=64) for i in range(2)]
@@ -95,9 +95,9 @@ def tile_list_tied_board_skip_tabled_kernel(
         pick_tokens(0)
         a_sb = [sb.tile([P, J], F32, name="a_sb%d" % t) for t in range(PACK)]
         a_ps = [ps.tile([P, J], F32, name="a_ps%d" % t) for t in range(PACK)]
-        for t in (0, 1, 3, 2):
+        for t in (0, 2, 1, 3):
             nc.tensor.matmul_mx(
-                out=a_ps[t][:], lhsT=w_w[t // 2][:, t % 2, :].bitcast(E5M2), lhsT_scale=w_s[:, t, :],
+                out=a_ps[t][:], lhsT=w_w[t % 2][:, t // 2, :].bitcast(E5M2), lhsT_scale=w_s[:, t, :],
                 rhs=xgw[0][:].bitcast(E2M1), rhs_scale=xgs[0][:], start=True, stop=True,
             )
         for t in (0, 1, 3):
@@ -108,7 +108,7 @@ def tile_list_tied_board_skip_tabled_kernel(
         p_ps = [ps.tile([P, 2, HALF], F32, name="p_ps%d" % h) for h in range(2)]
         for t in range(PACK):
             nc.tensor.matmul_mx(
-                out=b_ps[t % 2][:, t // 2, :], lhsT=w_w[t // 2][:, t % 2, :].bitcast(E5M2), lhsT_scale=w_s[:, t, :],
+                out=b_ps[t % 2][:, t // 2, :], lhsT=w_w[t % 2][:, t // 2, :].bitcast(E5M2), lhsT_scale=w_s[:, t, :],
                 rhs=xgw[1][:].bitcast(E2M1), rhs_scale=xgs[1][:], start=True, stop=True,
             )
         for h in range(2):
@@ -121,8 +121,8 @@ def tile_list_tied_board_skip_tabled_kernel(
                 )
 
         looked = [sb.tile([P, 2, J], F32, name="looked%d" % e) for e in range(2)]
-        nc.vector.tensor_copy(boards[0][:].indirect(lists[2][:]), a_sb[0][:])
         nc.vector.tensor_copy(a_sb[2][:], a_ps[2][:])
+        nc.vector.tensor_copy(boards[0][:].indirect(lists[2][:]), a_sb[0][:])
         nc.vector.tensor_copy(boards[2][:].indirect(lists[2][:]), a_sb[2][:])
         for t in (1, 3):
             nc.scalar.activation(boards[t][:].indirect(lists[2][:]), a_sb[t][:], ACT.Copy)
@@ -130,32 +130,23 @@ def tile_list_tied_board_skip_tabled_kernel(
             nc.vector.tensor_copy(looked[0][:, u, :], boards[2 * u][:].indirect(lists[3][:]))
             nc.scalar.activation(looked[1][:, u, :], boards[2 * u + 1][:].indirect(lists[3][:]), ACT.Copy)
 
-        tzg = sb.tile([P, 2, J], F32, tag="board3")
-        nc.scalar.activation(tzg[:, 0, :], tz_sb[0][:].indirect(lists[4][:]), ACT.Copy)
-        diff = sb.tile([P, 2, 2, 2, HALF], F32)
-        hid = [
-            sb.tile([P, HALF, PACK], BF16, name="hid0", tag="tz0", align_bytes=64),
-            sb.tile([P, HALF, PACK], BF16, name="hid1", align_bytes=64),
-        ]
-        nc.vector.tensor_tensor(
-            diff[:, :, :, 0, :],
-            looked[0][:].rearrange("p u (h j) -> p h u j", h=2),
-            b_ps[0][:].rearrange("p u (h j) -> p h u j", h=2),
-            ALU.subtract,
-        )
+        diff = [sb.tile([P, 2, 2, HALF], F32, name="diff%d" % h) for h in range(2)]
+        hid = [sb.tile([P, HALF, PACK], BF16, name="hid%d" % h, align_bytes=64) for h in range(2)]
+        for e in range(2):
+            for h in range(2):
+                cols = slice(h * HALF, (h + 1) * HALF)
+                nc.vector.tensor_tensor(diff[h][:, :, e, :], looked[e][:, :, cols], b_ps[e][:, :, cols], ALU.subtract)
         for h in range(2):
-            cols = slice(h * HALF, (h + 1) * HALF)
-            nc.vector.tensor_tensor(diff[:, h, :, 1, :], looked[1][:, :, cols], b_ps[1][:, :, cols], ALU.subtract)
             nc.scalar.activation(
                 hid[h][:].rearrange("p (c i) t -> p c t i", i=4),
-                diff[:, h, :, :, :].rearrange("p u e (c i) -> p c (u e) i", i=4),
+                diff[h][:].rearrange("p u e (c i) -> p c (u e) i", i=4),
                 ACT.Abs,
             )
-        nc.vector.tensor_copy(tzg[:, 1, :], tz_sb[1][:].indirect(lists[4][:]))
-        hq_w = [
-            sb.tile([P, HALF], U32, name="hq_w0", tag="tz1", align_bytes=64),
-            sb.tile([P, HALF], U32, name="hq_w1", align_bytes=64),
-        ]
+        tzg = sb.tile([P, 2, 2, HALF], F32, tag="looked1")
+        for n in range(2):
+            nc.vector.tensor_copy(tzg[:, 0, n, :], tz_sb[n][:].indirect(lists[4][:, 0:8]))
+            nc.scalar.activation(tzg[:, 1, n, :], tz_sb[n][:].indirect(lists[4][:, 8:16]), ACT.Copy)
+        hq_w = [sb.tile([P, HALF], U32, name="hq_w%d" % h, align_bytes=64) for h in range(2)]
         hq_s = [sb.tile([P, HALF], U8, name="hq_s%d" % h, align_bytes=64) for h in range(2)]
         for h in range(2):
             nc.vector.quantize_mx(
@@ -171,5 +162,5 @@ def tile_list_tied_board_skip_tabled_kernel(
         for h in range(2):
             cols = slice(h * HALF, (h + 1) * HALF)
             y = sb.tile([P, 2, HALF], F32, name="y%d" % h, tag="hid1" if h == 0 else "y1", align_bytes=64)
-            nc.vector.tensor_tensor(y[:], p_ps[h][:], tzg[:, :, cols], ALU.add)
+            nc.vector.tensor_tensor(y[:], p_ps[h][:], tzg[:, h, :, :], ALU.add)
             nc.sync.dma_start(out=out_v[:, :, cols], in_=y[:])

from contextlib import ExitStack

import concourse.mybir as mybir

K, T, J, R, C, N, E = 512, 2048, 256, 512, 512, 256, 1024
FLOPS = 2 * K * R * J * 2 + 2 * R * N * J + 2 * K * N * J

F32 = mybir.dt.float32
BF16 = mybir.dt.bfloat16
I32 = mybir.dt.int32
U32 = mybir.dt.uint32
U16 = mybir.dt.uint16
U8 = mybir.dt.uint8
E2M1 = mybir.dt.float4_e2m1fn_x4
E4M3 = mybir.dt.float8_e4m3fn_x4
E5M2 = mybir.dt.float8_e5m2_x4
ACT = mybir.ActivationFunctionType
ALU = mybir.AluOpType

P = 128
PACK = 4
HALF = J // 2


def load_plane(eng, plane, scales):
    for q in range(4):
        eng.dma_start(out=plane[32 * q : 32 * q + 4, :].bitcast(I32), in_=scales[0, 4 * q : 4 * q + 4, :].bitcast(I32))


def words_of(dram):
    return dram[0].rearrange("p n t -> p (n t)").bitcast(I32)


def tile_list_tied_board_skip_tabled_kernel(
    tc, xt_words, xt_scales, w_words, w_scales, wb_words, wb_scales, ws_words, ws_scales, tz,
    offs, offs2, offs3, offs4, offs5, out,
):
    nc = tc.nc
    with ExitStack() as ctx:
        sb = ctx.enter_context(tc.tile_pool(name="sb", bufs=1))
        ps = ctx.enter_context(tc.psum_pool(name="ps", bufs=1))

        lists = [sb.tile([P, J // 16], U16, name="list%d" % i) for i in range(5)]
        xw = sb.tile([P, T], U16, align_bytes=64)
        xs = sb.tile([P, T], U8, align_bytes=64)
        w_raw = sb.tile([P, R], U32, align_bytes=64)
        wsc_raw = sb.tile([P, R], U8, align_bytes=64)
        wb_w = sb.tile([P, N], U32, align_bytes=64)
        wb_s = sb.tile([P, N], U8, align_bytes=64)
        ws_w = sb.tile([P, N], U32, align_bytes=64)
        ws_s = sb.tile([P, N], U8, align_bytes=64)
        tz_sb = [sb.tile([P, E], F32, name="tz%d" % h, align_bytes=64) for h in range(2)]
        boards = [sb.tile([P, C], F32, name="board%d" % t) for t in range(PACK)]

        nc.vector.memset(wsc_raw[:].bitcast(I32), 0)
        nc.vector.memset(xs[:, : T // 2].bitcast(I32), 0)
        nc.gpsimd.memset(xs[:, T // 2 :].bitcast(I32), 0)
        for t in range(PACK):
            nc.vector.memset(boards[t][:], 0.0)
        nc.gpsimd.memset(ws_s[:].bitcast(I32), 0)
        nc.gpsimd.memset(wb_s[:].bitcast(I32), 0)

        nc.sync.dma_start(lists[0][:], offs)
        nc.sync.dma_start(lists[1][:], offs2)
        load_plane(nc.sync, wsc_raw, w_scales)
        nc.sync.dma_start(out=xw[:].bitcast(I32), in_=xt_words[0].bitcast(I32))
        nc.sync.dma_start(out=w_raw[:].bitcast(I32), in_=words_of(w_words))
        load_plane(nc.sync, xs, xt_scales)
        nc.sync.dma_start(lists[2][:], offs3)
        nc.sync.dma_start(lists[3][:], offs4)
        nc.sync.dma_start(lists[4][:], offs5)
        for n in range(2):
            nc.sync.dma_start(out=tz_sb[n][:], in_=tz[n * P : (n + 1) * P, :])
        nc.sync.dma_start(out=ws_w[:].bitcast(I32), in_=words_of(ws_words))
        nc.sync.dma_start(out=wb_w[:].bitcast(I32), in_=words_of(wb_words))
        load_plane(nc.sync, ws_s, ws_scales)
        load_plane(nc.sync, wb_s, wb_scales)

        w_w = [sb.tile([P, 2, P], U32, name="w_w%d" % u, align_bytes=64) for u in range(2)]
        w_s = sb.tile([P, PACK, P], U8, align_bytes=64)
        nc.vector.tensor_copy(out=w_s[:], in_=wsc_raw[:].rearrange("p (m t) -> p t m", t=PACK))
        for u in range(2):
            nc.scalar.copy(
                out=w_w[u][:].rearrange("p t (c i) -> p c t i", i=4),
                in_=w_raw[:].rearrange("p (c i v e) -> p e c v i", i=4, v=2, e=2)[:, u, :, :, :],
            )

        xgw = [sb.tile([P, J], U16, name="xgw%d" % i, align_bytes=64) for i in range(2)]
        xgs = [sb.tile([P, J], U8, name="xgs%d" % i, align_bytes=64) for i in range(2)]

        def pick_tokens(i):
            nc.vector.tensor_copy(xgw[i][:], xw[:].indirect(lists[i][:]))
            nc.vector.tensor_copy(xgs[i][:], xs[:].indirect(lists[i][:]))

        pick_tokens(0)
        a_sb = [sb.tile([P, J], F32, name="a_sb%d" % t) for t in range(PACK)]
        a_ps = [ps.tile([P, J], F32, name="a_ps%d" % t) for t in range(PACK)]
        for t in (0, 2, 1, 3):
            nc.tensor.matmul_mx(
                out=a_ps[t][:], lhsT=w_w[t % 2][:, t // 2, :].bitcast(E5M2), lhsT_scale=w_s[:, t, :],
                rhs=xgw[0][:].bitcast(E2M1), rhs_scale=xgs[0][:], start=True, stop=True,
            )
        for t in (0, 1, 3):
            nc.scalar.activation(a_sb[t][:], a_ps[t][:], ACT.Copy)

        pick_tokens(1)
        b_ps = [ps.tile([P, 2, J], F32, name="b_ps%d" % e) for e in range(2)]
        p_ps = [ps.tile([P, 2, HALF], F32, name="p_ps%d" % h) for h in range(2)]
        for t in range(PACK):
            nc.tensor.matmul_mx(
                out=b_ps[t % 2][:, t // 2, :], lhsT=w_w[t % 2][:, t // 2, :].bitcast(E5M2), lhsT_scale=w_s[:, t, :],
                rhs=xgw[1][:].bitcast(E2M1), rhs_scale=xgs[1][:], start=True, stop=True,
            )
        for h in range(2):
            cols = slice(h * HALF, (h + 1) * HALF)
            for n in range(2):
                rows = slice(n * P, (n + 1) * P)
                nc.tensor.matmul_mx(
                    out=p_ps[h][:, n, :], lhsT=ws_w[:, rows].bitcast(E4M3), lhsT_scale=ws_s[:, rows],
                    rhs=xgw[1][:, cols].bitcast(E2M1), rhs_scale=xgs[1][:, cols], start=(n == 0), stop=False,
                )

        looked = [sb.tile([P, 2, J], F32, name="looked%d" % e) for e in range(2)]
        nc.vector.tensor_copy(a_sb[2][:], a_ps[2][:])
        nc.vector.tensor_copy(boards[0][:].indirect(lists[2][:]), a_sb[0][:])
        nc.vector.tensor_copy(boards[2][:].indirect(lists[2][:]), a_sb[2][:])
        for t in (1, 3):
            nc.scalar.activation(boards[t][:].indirect(lists[2][:]), a_sb[t][:], ACT.Copy)
        for u in range(2):
            nc.vector.tensor_copy(looked[0][:, u, :], boards[2 * u][:].indirect(lists[3][:]))
            nc.scalar.activation(looked[1][:, u, :], boards[2 * u + 1][:].indirect(lists[3][:]), ACT.Copy)

        diff = [sb.tile([P, 2, 2, HALF], F32, name="diff%d" % h) for h in range(2)]
        hid = [sb.tile([P, HALF, PACK], BF16, name="hid%d" % h, align_bytes=64) for h in range(2)]
        for e in range(2):
            for h in range(2):
                cols = slice(h * HALF, (h + 1) * HALF)
                nc.vector.tensor_tensor(diff[h][:, :, e, :], looked[e][:, :, cols], b_ps[e][:, :, cols], ALU.subtract)
        for h in range(2):
            nc.scalar.activation(
                hid[h][:].rearrange("p (c i) t -> p c t i", i=4),
                diff[h][:].rearrange("p u e (c i) -> p c (u e) i", i=4),
                ACT.Abs,
            )
        tzg = sb.tile([P, 2, 2, HALF], F32, tag="looked1")
        for n in range(2):
            nc.vector.tensor_copy(tzg[:, 0, n, :], tz_sb[n][:].indirect(lists[4][:, 0:8]))
            nc.scalar.activation(tzg[:, 1, n, :], tz_sb[n][:].indirect(lists[4][:, 8:16]), ACT.Copy)
        hq_w = [sb.tile([P, HALF], U32, name="hq_w%d" % h, align_bytes=64) for h in range(2)]
        hq_s = [sb.tile([P, HALF], U8, name="hq_s%d" % h, align_bytes=64) for h in range(2)]
        for h in range(2):
            nc.vector.quantize_mx(
                out=hq_w[h][:].bitcast(E5M2), scales=hq_s[h][:], in_=hid[h][:].rearrange("p j t -> p (j t)")
            )
            for n in range(2):
                rows = slice(n * P, (n + 1) * P)
                nc.tensor.matmul_mx(
                    out=p_ps[h][:, n, :], lhsT=wb_w[:, rows].bitcast(E4M3), lhsT_scale=wb_s[:, rows],
                    rhs=hq_w[h][:].bitcast(E5M2), rhs_scale=hq_s[h][:], start=False, stop=(n == 1),
                )
        out_v = out.rearrange("(n p) j -> p n j", p=P)
        for h in range(2):
            cols = slice(h * HALF, (h + 1) * HALF)
            y = sb.tile([P, 2, HALF], F32, name="y%d" % h, tag="hid1" if h == 0 else "y1", align_bytes=64)
            nc.vector.tensor_tensor(y[:], p_ps[h][:], tzg[:, h, :, :], ALU.add)
            nc.sync.dma_start(out=out_v[:, :, cols], in_=y[:])
